import numpy as np
import ml_dtypes


def mxq(x, axis, fmt="e4m3"):
    dtype, down = {"e4m3": (ml_dtypes.float8_e4m3fn, 7), "e5m2": (ml_dtypes.float8_e5m2, 14)}[fmt]
    v = np.moveaxis(np.asarray(x, np.float32).astype(ml_dtypes.bfloat16).astype(np.float64), axis, -1)
    blocks = v.reshape(v.shape[:-1] + (-1, 32))
    amax = np.abs(blocks).max(-1, keepdims=True)
    byte = np.maximum(np.where(amax > 0, np.frexp(amax)[1] - 1 + 127, 0) - down, 1)
    scale = np.exp2(byte - 127.0)
    codes = (blocks / scale).astype(np.float32).astype(dtype).astype(np.float64)
    return np.moveaxis((codes * scale).reshape(v.shape), -1, axis)


WIDE = False


def mx_kscale(k):
    if not WIDE:
        return np.ones(k)
    levels = np.array([10, -10, 5, -5, 0])
    if k % 512:
        return np.exp2(np.random.permutation(np.resize(levels, k // 32))).repeat(32)
    a = np.empty((k // 512, 16))
    for p in range(k // 512):
        a[p, :8] = np.random.permutation(np.resize(levels, 8))
        for g in range(8):
            far = levels[np.abs(levels - a[p, g]) >= 10]
            a[p, g + 8] = far[np.random.randint(len(far))]
    return np.exp2(a.ravel()).repeat(32)


def f64(x):
    return np.asarray(x).astype(np.float64)


def striped8(idx):
    return np.asarray(idx).reshape(8, -1, 16).transpose(0, 2, 1).reshape(128, -1).astype(np.uint16)


def unstriped8(offs):
    return offs.reshape(8, 16, -1).transpose(0, 2, 1).reshape(8, -1).astype(np.int64)


def pick8(x, idx, run):
    r = np.arange(len(x))
    return x[r[:, None], idx[r % (8 * run) // run]]


E2M1 = np.array([0.0, 0.5, 1.0, 1.5, 2.0, 3.0, 4.0, 6.0, -0.0, -0.5, -1.0, -1.5, -2.0, -3.0, -4.0, -6.0])


def pack_weight(w, fmt):
    k, n = w.shape
    w = f64(np.asarray(w, np.float32).astype(ml_dtypes.bfloat16)).reshape(k // 32, 32, n)
    amax = np.abs(w).max(1)
    if fmt == "e4m3":
        byte = np.frexp(amax)[1] - 1 + 127 - 7
    else:
        mant, ex = np.frexp(amax / 6.0)
        byte = np.where(mant > 0.5, ex, ex - 1) + 127
    byte = np.clip(np.where(amax > 0, byte, 1), 1, 254)
    scaled = (w * np.exp2(127.0 - byte)[:, None, :]).reshape(k, n).astype(np.float32)
    by_word = np.ascontiguousarray(scaled.reshape(k // 512, 128, 4, n).transpose(0, 1, 3, 2))
    if fmt == "e4m3":
        words = by_word.astype(ml_dtypes.float8_e4m3fn).view(np.uint8)
    else:
        c = by_word.astype(ml_dtypes.float4_e2m1fn).view(np.uint8) & 0xF
        words = (c[..., 0::2] | (c[..., 1::2] << 4)).reshape(k // 512, 128, 2 * n)
    return np.ascontiguousarray(words), np.ascontiguousarray(byte.astype(np.uint8).reshape(k // 512, 16, n))


def unpack_weight(words, scales, fmt):
    g, _, n = scales.shape
    words = np.ascontiguousarray(words).reshape(g, 128, n, -1)
    if fmt == "e4m3":
        vals = words.view(ml_dtypes.float8_e4m3fn).astype(np.float64)
    else:
        nib = np.empty((g, 128, n, 4), np.uint8)
        nib[..., 0::2] = words & 0xF
        nib[..., 1::2] = words >> 4
        vals = E2M1[nib]
    vals = vals * np.repeat(np.exp2(scales.astype(np.float64) - 127.0), 8, axis=1)[..., None]
    return vals.transpose(0, 1, 3, 2).reshape(g * 512, n)


D, T, U, I, Q = 512, 1024, 1024, 512, 128


def setup_inputs():
    n = np.random.standard_normal
    idx = np.stack([np.random.permutation(T)[:I] for _ in range(8)])
    idx2 = np.stack([np.random.permutation(U)[:I] for _ in range(8)])
    idx3 = np.stack([np.random.permutation(U)[:I] for _ in range(8)])
    idx4 = np.stack([np.random.permutation(T)[:I] for _ in range(8)])
    fd = mx_kscale(D)
    keysp = pack_weight(n((D, T)) / fd[:, None], "e2m1")
    notesp = pack_weight(n((D, U)) / fd[:, None], "e4m3")
    return {
        "query": (n((D, Q)) * 1.0 / np.sqrt(D) * fd[:, None]).astype(np.float32),
        "keys_words": keysp[0],
        "keys_scales": keysp[1],
        "notes_words": notesp[0],
        "notes_scales": notesp[1],
        "lam": (np.random.uniform(0.5, 1.5, (Q, 1))).astype(np.float32),
        "offs": striped8(idx),
        "offs2": striped8(idx2),
        "offs3": striped8(idx3),
        "offs4": striped8(idx4),
    }


def reference(query, keys_words, keys_scales, notes_words, notes_scales, lam, offs, offs2, offs3, offs4):
    idx = unstriped8(offs)
    idx2 = unstriped8(offs2)
    idx3 = unstriped8(offs3)
    idx4 = unstriped8(offs4)
    keysu = unpack_weight(keys_words, keys_scales, "e2m1")
    notesu = unpack_weight(notes_words, notes_scales, "e4m3")
    queryq = mxq(f64(query), 0, "e4m3")
    a = queryq.T @ keysu
    b = queryq.T @ notesu
    w = pick8(a, idx, 16) - pick8(b, idx2, 16)
    f1 = np.zeros((Q, U))
    f1[np.arange(Q)[:, None], idx3[np.arange(Q) % 128 // 16]] = w
    bb = b + f1 * f64(lam)
    y = pick8(bb, idx2, 16) + pick8(a, idx4, 16)
    return y

@@ -1,0 +1,123 @@
+from contextlib import ExitStack
+
+import concourse.mybir as mybir
+
+F32 = mybir.dt.float32
+BF16 = mybir.dt.bfloat16
+I32 = mybir.dt.int32
+U32 = mybir.dt.uint32
+U16 = mybir.dt.uint16
+U8 = mybir.dt.uint8
+FP8X4 = mybir.dt.float8_e4m3fn_x4
+FP4X4 = mybir.dt.float4_e2m1fn_x4
+MULT = mybir.AluOpType.mult
+ADD = mybir.AluOpType.add
+COPY = mybir.ActivationFunctionType.Copy
+
+P = 128
+PACK = 4
+D, POOL, SLOTS, Q = 512, 1024, 512, 128
+N = 256
+HALF = SLOTS // 2
+LIST_HALF = HALF // 16
+NOTES_PLANE = 4
+
+FLOPS = 2 * D * Q * 2 * POOL
+
+
+def load_scale_rows(queue, plane, scales, first, which):
+    rows = scales[0].bitcast(I32).rearrange("(quad r) c -> r quad c", r=4)
+    for r in which:
+        queue.dma_start(out=plane[first + r : P : 32, :].bitcast(I32), in_=rows[r])
+
+
+def tile_attend_followers_two_kernel(tc, query, keys_words, keys_scales, notes_words, notes_scales, lam, offs, offs2, offs3, offs4, out):
+    nc = tc.nc
+    with ExitStack() as ctx:
+        sb = ctx.enter_context(tc.tile_pool(name="sb", bufs=1))
+        ps = ctx.enter_context(tc.psum_pool(name="ps", bufs=1))
+
+        q_raw = sb.tile([P, PACK, Q], F32, name="q_raw")
+        q_bf = sb.tile([P, Q, PACK], BF16, name="q_bf", align_bytes=64)
+        q_codes = sb.tile([P, Q], U32, name="q_codes", align_bytes=64)
+        q_plane = sb.tile([P, Q], U8, name="q_plane", align_bytes=64)
+        k_words = sb.tile([P, 2 * POOL], U8, name="k_words", align_bytes=64)
+        k_plane = sb.tile([P, POOL], U8, name="k_plane", align_bytes=64)
+        n_words = sb.tile([P, POOL], U32, name="n_words", align_bytes=64)
+        n_plane = sb.tile([P, POOL], U8, name="n_plane", align_bytes=64)
+        lam_col = sb.tile([P, 1], F32, name="lam_col")
+        idx = sb.tile([P, SLOTS // 16], U16, name="idx")
+        idx2 = sb.tile([P, SLOTS // 16], U16, name="idx2")
+        idx3 = sb.tile([P, SLOTS // 16], U16, name="idx3")
+        idx4 = sb.tile([P, SLOTS // 16], U16, name="idx4")
+        a = sb.tile([P, POOL], F32, name="a")
+        b = sb.tile([P, POOL], F32, name="b")
+        f1 = sb.tile([P, POOL], F32, name="f1")
+        bb = sb.tile([P, POOL], F32, name="bb")
+        a_lead = sb.tile([P, SLOTS], F32, name="a_lead")
+        b_neg = sb.tile([P, SLOTS], F32, name="b_neg")
+        a_last = sb.tile([P, SLOTS], F32, name="a_last")
+        bb_high = sb.tile([P, HALF], F32, name="bb_high")
+        y_low = sb.tile([P, HALF], F32, name="y_low")
+        y_high = sb.tile([P, HALF], F32, name="y_high")
+
+        nc.vector.memset(k_plane[:].bitcast(U32), 0)
+        nc.gpsimd.memset(n_plane[:].bitcast(U32), 0)
+        nc.vector.memset(f1[:], 0.0)
+
+        nc.sync.dma_start(out=q_raw[:], in_=query.rearrange("(p j) w -> p j w", j=PACK))
+        load_scale_rows(nc.sync, k_plane, keys_scales, 0, range(4))
+        nc.sync.dma_start(out=k_words[:].bitcast(I32), in_=keys_words[0].bitcast(I32))
+        load_scale_rows(nc.sync, n_plane, notes_scales, NOTES_PLANE, range(1))
+        nc.sync.dma_start(out=n_words[:].bitcast(I32), in_=notes_words[0].rearrange("p n t -> p (n t)").bitcast(I32))
+        load_scale_rows(nc.sync, n_plane, notes_scales, NOTES_PLANE, range(1, 4))
+        nc.sync.dma_start(idx[:], offs)
+        nc.sync.dma_start(idx2[:], offs2)
+        nc.sync.dma_start(idx3[:], offs3)
+        nc.sync.dma_start(idx4[:], offs4)
+        nc.sync.dma_start(lam_col[:], lam)
+
+        nc.vector.tensor_copy(out=q_bf[:], in_=q_raw[:].rearrange("p j w -> p w j"))
+        nc.vector.quantize_mx(out=q_codes[:].bitcast(FP8X4), scales=q_plane[:], in_=q_bf[:].rearrange("p w j -> p (w j)"))
+
+        for c in range(POOL // N):
+            cols = slice(c * N, (c + 1) * N)
+            bank = ps.tile([P, N], F32, name=f"bank_a{c}")
+            nc.tensor.matmul_mx(
+                out=bank[:],
+                lhsT=q_codes[:].bitcast(FP8X4),
+                lhsT_scale=q_plane[:],
+                rhs=k_words[:, 2 * c * N : 2 * (c + 1) * N].bitcast(FP4X4),
+                rhs_scale=k_plane[:, cols],
+                start=True,
+                stop=True,
+            )
+            if c % 2 == 1:
+                nc.scalar.activation(a[:, cols], bank[:], COPY)
+            else:
+                nc.vector.tensor_copy(out=a[:, cols], in_=bank[:])
+        nc.scalar.activation(a_lead[:], a[:].indirect(idx[:]), COPY)
+        for c in range(POOL // N):
+            cols = slice(c * N, (c + 1) * N)
+            bank = ps.tile([P, N], F32, name=f"bank_b{c}")
+            nc.tensor.matmul_mx(
+                out=bank[:],
+                lhsT=q_codes[:].bitcast(FP8X4),
+                lhsT_scale=q_plane[:],
+                rhs=n_words[:, cols].bitcast(FP8X4),
+                rhs_scale=n_plane[NOTES_PLANE:P, cols],
+                start=True,
+                stop=True,
+            )
+            nc.vector.tensor_copy(out=b[:, cols], in_=bank[:])
+
+        nc.vector.tensor_scalar(b_neg[:, :HALF], b[:].indirect(idx2[:, :LIST_HALF]), -1.0, 0.0, MULT, ADD)
+        nc.scalar.activation(b_neg[:, HALF:], b[:].indirect(idx2[:, LIST_HALF:]), COPY, scale=-1.0)
+        nc.vector.tensor_tensor(f1[:].indirect(idx3[:]), a_lead[:], b_neg[:], ADD)
+        nc.scalar.activation(a_last[:], a[:].indirect(idx4[:]), COPY)
+        nc.vector.scalar_tensor_tensor(bb[:], f1[:], lam_col[:], b[:], MULT, ADD)
+        nc.vector.tensor_tensor(y_low[:], bb[:].indirect(idx2[:, :LIST_HALF]), a_last[:, :HALF], ADD)
+        nc.scalar.activation(bb_high[:], bb[:].indirect(idx2[:, LIST_HALF:]), COPY)
+        nc.sync.dma_start(out=out[:, :HALF], in_=y_low[:])
+        nc.vector.tensor_tensor(y_high[:], bb_high[:], a_last[:, HALF:], ADD)
+        nc.scalar.dma_start(out=out[:, HALF:], in_=y_high[:])

@@ -62,22 +62,24 @@ def tile_attend_followers_two_kernel(tc, query, keys_words, keys_scales, notes_w
         y_high = sb.tile([P, HALF], F32, name="y_high")
 
         nc.vector.memset(k_plane[:].bitcast(U32), 0)
-        nc.gpsimd.memset(n_plane[:].bitcast(U32), 0)
+        nc.vector.memset(n_plane[:].bitcast(U32), 0)
         nc.vector.memset(f1[:], 0.0)
 
         nc.sync.dma_start(out=q_raw[:], in_=query.rearrange("(p j) w -> p j w", j=PACK))
-        load_scale_rows(nc.sync, k_plane, keys_scales, 0, range(4))
-        nc.sync.dma_start(out=k_words[:].bitcast(I32), in_=keys_words[0].bitcast(I32))
-        load_scale_rows(nc.sync, n_plane, notes_scales, NOTES_PLANE, range(1))
-        nc.sync.dma_start(out=n_words[:].bitcast(I32), in_=notes_words[0].rearrange("p n t -> p (n t)").bitcast(I32))
-        load_scale_rows(nc.sync, n_plane, notes_scales, NOTES_PLANE, range(1, 4))
         nc.sync.dma_start(idx[:], offs)
+        load_scale_rows(nc.sync, k_plane, keys_scales, 0, (0, 1))
+        nc.sync.dma_start(out=k_words[:].bitcast(I32), in_=keys_words[0].bitcast(I32))
+        load_scale_rows(nc.sync, k_plane, keys_scales, 0, (2, 3))
+        nc.sync.dma_start(out=n_words[:].bitcast(I32), in_=notes_words[0].rearrange("p n t -> p (n t)").bitcast(I32))
+        load_scale_rows(nc.sync, n_plane, notes_scales, NOTES_PLANE, range(4))
         nc.sync.dma_start(idx2[:], offs2)
         nc.sync.dma_start(idx3[:], offs3)
         nc.sync.dma_start(idx4[:], offs4)
         nc.sync.dma_start(lam_col[:], lam)
 
-        nc.vector.tensor_copy(out=q_bf[:], in_=q_raw[:].rearrange("p j w -> p w j"))
+        q_cols = q_raw[:].rearrange("p j w -> p w j")
+        nc.vector.tensor_copy(out=q_bf[:, : Q // 2, :], in_=q_cols[:, : Q // 2, :])
+        nc.scalar.activation(q_bf[:, Q // 2 :, :], q_cols[:, Q // 2 :, :], COPY)
         nc.vector.quantize_mx(out=q_codes[:].bitcast(FP8X4), scales=q_plane[:], in_=q_bf[:].rearrange("p w j -> p (w j)"))
 
         for c in range(POOL // N):
@@ -96,7 +98,7 @@ def tile_attend_followers_two_kernel(tc, query, keys_words, keys_scales, notes_w
                 nc.scalar.activation(a[:, cols], bank[:], COPY)
             else:
                 nc.vector.tensor_copy(out=a[:, cols], in_=bank[:])
-        nc.scalar.activation(a_lead[:], a[:].indirect(idx[:]), COPY)
+        nc.vector.tensor_copy(a_lead[:], a[:].indirect(idx[:]))
         for c in range(POOL // N):
             cols = slice(c * N, (c + 1) * N)
             bank = ps.tile([P, N], F32, name=f"bank_b{c}")
@@ -109,7 +111,7 @@ def tile_attend_followers_two_kernel(tc, query, keys_words, keys_scales, notes_w
                 start=True,
                 stop=True,
             )
-            nc.vector.tensor_copy(out=b[:, cols], in_=bank[:])
+            nc.scalar.activation(b[:, cols], bank[:], COPY)
 
         nc.vector.tensor_scalar(b_neg[:, :HALF], b[:].indirect(idx2[:, :LIST_HALF]), -1.0, 0.0, MULT, ADD)
         nc.scalar.activation(b_neg[:, HALF:], b[:].indirect(idx2[:, LIST_HALF:]), COPY, scale=-1.0)
@@ -120,4 +122,4 @@ def tile_attend_followers_two_kernel(tc, query, keys_words, keys_scales, notes_w
         nc.scalar.activation(bb_high[:], bb[:].indirect(idx2[:, LIST_HALF:]), COPY)
         nc.sync.dma_start(out=out[:, :HALF], in_=y_low[:])
         nc.vector.tensor_tensor(y_high[:], bb_high[:], a_last[:, HALF:], ADD)
-        nc.scalar.dma_start(out=out[:, HALF:], in_=y_high[:])
+        nc.sync.dma_start(out=out[:, HALF:], in_=y_high[:])

from contextlib import ExitStack

import concourse.mybir as mybir

F32 = mybir.dt.float32
BF16 = mybir.dt.bfloat16
I32 = mybir.dt.int32
U32 = mybir.dt.uint32
U16 = mybir.dt.uint16
U8 = mybir.dt.uint8
FP8X4 = mybir.dt.float8_e4m3fn_x4
FP4X4 = mybir.dt.float4_e2m1fn_x4
MULT = mybir.AluOpType.mult
ADD = mybir.AluOpType.add
COPY = mybir.ActivationFunctionType.Copy

P = 128
PACK = 4
D, POOL, SLOTS, Q = 512, 1024, 512, 128
N = 256
HALF = SLOTS // 2
LIST_HALF = HALF // 16
NOTES_PLANE = 4

FLOPS = 2 * D * Q * 2 * POOL


def load_scale_rows(queue, plane, scales, first, which):
    rows = scales[0].bitcast(I32).rearrange("(quad r) c -> r quad c", r=4)
    for r in which:
        queue.dma_start(out=plane[first + r : P : 32, :].bitcast(I32), in_=rows[r])


def tile_attend_followers_two_kernel(tc, query, keys_words, keys_scales, notes_words, notes_scales, lam, offs, offs2, offs3, offs4, out):
    nc = tc.nc
    with ExitStack() as ctx:
        sb = ctx.enter_context(tc.tile_pool(name="sb", bufs=1))
        ps = ctx.enter_context(tc.psum_pool(name="ps", bufs=1))

        q_raw = sb.tile([P, PACK, Q], F32, name="q_raw")
        q_bf = sb.tile([P, Q, PACK], BF16, name="q_bf", align_bytes=64)
        q_codes = sb.tile([P, Q], U32, name="q_codes", align_bytes=64)
        q_plane = sb.tile([P, Q], U8, name="q_plane", align_bytes=64)
        k_words = sb.tile([P, 2 * POOL], U8, name="k_words", align_bytes=64)
        k_plane = sb.tile([P, POOL], U8, name="k_plane", align_bytes=64)
        n_words = sb.tile([P, POOL], U32, name="n_words", align_bytes=64)
        n_plane = sb.tile([P, POOL], U8, name="n_plane", align_bytes=64)
        lam_col = sb.tile([P, 1], F32, name="lam_col")
        idx = sb.tile([P, SLOTS // 16], U16, name="idx")
        idx2 = sb.tile([P, SLOTS // 16], U16, name="idx2")
        idx3 = sb.tile([P, SLOTS // 16], U16, name="idx3")
        idx4 = sb.tile([P, SLOTS // 16], U16, name="idx4")
        a = sb.tile([P, POOL], F32, name="a")
        b = sb.tile([P, POOL], F32, name="b")
        f1 = sb.tile([P, POOL], F32, name="f1")
        bb = sb.tile([P, POOL], F32, name="bb")
        a_lead = sb.tile([P, SLOTS], F32, name="a_lead")
        b_neg = sb.tile([P, SLOTS], F32, name="b_neg")
        a_last = sb.tile([P, SLOTS], F32, name="a_last")
        bb_high = sb.tile([P, HALF], F32, name="bb_high")
        y_low = sb.tile([P, HALF], F32, name="y_low")
        y_high = sb.tile([P, HALF], F32, name="y_high")

        nc.vector.memset(k_plane[:].bitcast(U32), 0)
        nc.vector.memset(n_plane[:].bitcast(U32), 0)
        nc.vector.memset(f1[:], 0.0)

        nc.sync.dma_start(out=q_raw[:], in_=query.rearrange("(p j) w -> p j w", j=PACK))
        nc.sync.dma_start(idx[:], offs)
        load_scale_rows(nc.sync, k_plane, keys_scales, 0, (0, 1))
        nc.sync.dma_start(out=k_words[:].bitcast(I32), in_=keys_words[0].bitcast(I32))
        load_scale_rows(nc.sync, k_plane, keys_scales, 0, (2, 3))
        nc.sync.dma_start(out=n_words[:].bitcast(I32), in_=notes_words[0].rearrange("p n t -> p (n t)").bitcast(I32))
        load_scale_rows(nc.sync, n_plane, notes_scales, NOTES_PLANE, range(4))
        nc.sync.dma_start(idx2[:], offs2)
        nc.sync.dma_start(idx3[:], offs3)
        nc.sync.dma_start(idx4[:], offs4)
        nc.sync.dma_start(lam_col[:], lam)

        q_cols = q_raw[:].rearrange("p j w -> p w j")
        nc.vector.tensor_copy(out=q_bf[:, : Q // 2, :], in_=q_cols[:, : Q // 2, :])
        nc.scalar.activation(q_bf[:, Q // 2 :, :], q_cols[:, Q // 2 :, :], COPY)
        nc.vector.quantize_mx(out=q_codes[:].bitcast(FP8X4), scales=q_plane[:], in_=q_bf[:].rearrange("p w j -> p (w j)"))

        for c in range(POOL // N):
            cols = slice(c * N, (c + 1) * N)
            bank = ps.tile([P, N], F32, name=f"bank_a{c}")
            nc.tensor.matmul_mx(
                out=bank[:],
                lhsT=q_codes[:].bitcast(FP8X4),
                lhsT_scale=q_plane[:],
                rhs=k_words[:, 2 * c * N : 2 * (c + 1) * N].bitcast(FP4X4),
                rhs_scale=k_plane[:, cols],
                start=True,
                stop=True,
            )
            if c % 2 == 1:
                nc.scalar.activation(a[:, cols], bank[:], COPY)
            else:
                nc.vector.tensor_copy(out=a[:, cols], in_=bank[:])
        nc.vector.tensor_copy(a_lead[:], a[:].indirect(idx[:]))
        for c in range(POOL // N):
            cols = slice(c * N, (c + 1) * N)
            bank = ps.tile([P, N], F32, name=f"bank_b{c}")
            nc.tensor.matmul_mx(
                out=bank[:],
                lhsT=q_codes[:].bitcast(FP8X4),
                lhsT_scale=q_plane[:],
                rhs=n_words[:, cols].bitcast(FP8X4),
                rhs_scale=n_plane[NOTES_PLANE:P, cols],
                start=True,
                stop=True,
            )
            nc.scalar.activation(b[:, cols], bank[:], COPY)

        nc.vector.tensor_scalar(b_neg[:, :HALF], b[:].indirect(idx2[:, :LIST_HALF]), -1.0, 0.0, MULT, ADD)
        nc.scalar.activation(b_neg[:, HALF:], b[:].indirect(idx2[:, LIST_HALF:]), COPY, scale=-1.0)
        nc.vector.tensor_tensor(f1[:].indirect(idx3[:]), a_lead[:], b_neg[:], ADD)
        nc.scalar.activation(a_last[:], a[:].indirect(idx4[:]), COPY)
        nc.vector.scalar_tensor_tensor(bb[:], f1[:], lam_col[:], b[:], MULT, ADD)
        nc.vector.tensor_tensor(y_low[:], bb[:].indirect(idx2[:, :LIST_HALF]), a_last[:, :HALF], ADD)
        nc.scalar.activation(bb_high[:], bb[:].indirect(idx2[:, LIST_HALF:]), COPY)
        nc.sync.dma_start(out=out[:, :HALF], in_=y_low[:])
        nc.vector.tensor_tensor(y_high[:], bb_high[:], a_last[:, HALF:], ADD)
        nc.sync.dma_start(out=out[:, HALF:], in_=y_high[:])
